import numpy as np
import ml_dtypes


def mxq(x, axis, fmt="e4m3"):
    dtype, down = {"e4m3": (ml_dtypes.float8_e4m3fn, 7), "e5m2": (ml_dtypes.float8_e5m2, 14)}[fmt]
    v = np.moveaxis(np.asarray(x, np.float32).astype(ml_dtypes.bfloat16).astype(np.float64), axis, -1)
    blocks = v.reshape(v.shape[:-1] + (-1, 32))
    amax = np.abs(blocks).max(-1, keepdims=True)
    byte = np.maximum(np.where(amax > 0, np.frexp(amax)[1] - 1 + 127, 0) - down, 1)
    scale = np.exp2(byte - 127.0)
    codes = (blocks / scale).astype(np.float32).astype(dtype).astype(np.float64)
    return np.moveaxis((codes * scale).reshape(v.shape), -1, axis)


WIDE = False


def mx_kscale(k):
    if not WIDE:
        return np.ones(k)
    levels = np.array([10, -10, 5, -5, 0])
    if k % 512:
        return np.exp2(np.random.permutation(np.resize(levels, k // 32))).repeat(32)
    a = np.empty((k // 512, 16))
    for p in range(k // 512):
        a[p, :8] = np.random.permutation(np.resize(levels, 8))
        for g in range(8):
            far = levels[np.abs(levels - a[p, g]) >= 10]
            a[p, g + 8] = far[np.random.randint(len(far))]
    return np.exp2(a.ravel()).repeat(32)


def f64(x):
    return np.asarray(x).astype(np.float64)


def striped(idx):
    return np.tile(idx.reshape(-1, 16).T, (8, 1)).astype(np.uint16)


def unstriped(offs):
    return offs[:16].T.reshape(-1).astype(np.int64)


def pack_weight(w):
    k, n = w.shape
    w = f64(np.asarray(w, np.float32).astype(ml_dtypes.bfloat16)).reshape(k // 32, 32, n)
    amax = np.abs(w).max(1)
    byte = np.clip(np.where(amax > 0, np.frexp(amax)[1] - 1 + 127 - 7, 1), 1, 254)
    scaled = (w * np.exp2(127.0 - byte)[:, None, :]).reshape(k, n).astype(np.float32)
    words = np.ascontiguousarray(scaled.reshape(k // 512, 128, 4, n).transpose(0, 1, 3, 2)).astype(ml_dtypes.float8_e4m3fn).view(np.uint8)
    return words, np.ascontiguousarray(byte.astype(np.uint8).reshape(k // 512, 16, n))


def unpack_weight(words, scales):
    g, p, n, _ = words.shape
    vals = np.ascontiguousarray(words).view(ml_dtypes.float8_e4m3fn).astype(np.float64) * np.repeat(np.exp2(scales.astype(np.float64) - 127.0), 8, axis=1)[..., None]
    return vals.transpose(0, 1, 3, 2).reshape(g * 512, n)


K, T, S, N, U = 1024, 2048, 1024, 128, 2048


def setup_inputs():
    n = np.random.standard_normal
    s = mx_kscale(K)[:, None]
    packed_xT = pack_weight(n((K, T)) * s)
    return {
        "x_words": packed_xT[0],
        "x_scales": packed_xT[1],
        "mem": n((N, U)).astype(np.float32),
        "w1": (n((K, N)) / np.sqrt(K) / s).astype(np.float32),
        "offs": striped(np.random.permutation(T)[:S]),
        "slot": striped(np.random.permutation(U)[:S]),
    }


def reference(x_words, x_scales, mem, w1, offs, slot):
    xq = unpack_weight(x_words, x_scales)[:, unstriped(offs)]
    y = mxq(f64(w1), 0, "e4m3").T @ xq
    out = f64(mem).copy()
    out[:, unstriped(slot)] = np.maximum(f64(mem)[:, unstriped(slot)], y)
    return out

@@ -1,0 +1,99 @@
+from contextlib import ExitStack
+
+import concourse.mybir as mybir
+
+K, T, S, N, U = 1024, 2048, 1024, 128, 2048
+FLOPS = 2 * K * N * S
+
+F32 = mybir.dt.float32
+BF16 = mybir.dt.bfloat16
+I32 = mybir.dt.int32
+U32 = mybir.dt.uint32
+U16 = mybir.dt.uint16
+U8 = mybir.dt.uint8
+FP8X4 = mybir.dt.float8_e4m3fn_x4
+
+P = 128
+PACK = 4
+PASSES = K // (P * PACK)
+BANK = 512
+LANES = 16
+
+
+def tile_picked_idxput_max_p_kernel(tc, x_words, x_scales, mem, w1, offs, slot, out):
+    nc = tc.nc
+    halves = S // BANK
+    with ExitStack() as ctx:
+        keep = ctx.enter_context(tc.tile_pool(name="keep", bufs=1))
+        psum = ctx.enter_context(tc.psum_pool(name="psum", bufs=1))
+
+        offs_sb = keep.tile([P, S // LANES], U16, name="offs_sb")
+        slot_sb = keep.tile([P, S // LANES], U16, name="slot_sb")
+        scales_all = keep.tile([P, T], U8, name="scales_all", align_bytes=64)
+        words_all = [keep.tile([P, T], U32, name="words_all%d" % z, align_bytes=64) for z in range(PASSES)]
+        w_raw = keep.tile([P, PASSES, PACK, N], F32, name="w_raw", align_bytes=64)
+        store = keep.tile([P, U], F32, name="store", align_bytes=64)
+
+        nc.vector.memset(scales_all[:].bitcast(I32), 0)
+        nc.sync.dma_start(offs_sb[:], offs)
+        for q in range(4):
+            nc.sync.dma_start(
+                out=scales_all[32 * q : 32 * q + 4 * PASSES, :].bitcast(I32),
+                in_=x_scales[:, 4 * q : 4 * q + 4, :].bitcast(I32),
+            )
+        for z in range(PASSES):
+            nc.sync.dma_start(
+                out=words_all[z][:].bitcast(I32),
+                in_=x_words[z].rearrange("p n t -> p (n t)").bitcast(I32),
+            )
+        nc.sync.dma_start(out=w_raw[:], in_=w1.rearrange("(z p j) m -> p z j m", z=PASSES, j=PACK))
+        nc.sync.dma_start(slot_sb[:], slot)
+        nc.sync.dma_start(out=store[:], in_=mem)
+
+        scales_picked = keep.tile([P, S], U8, name="scales_picked", align_bytes=64)
+        nc.vector.tensor_copy(scales_picked[:], scales_all[:].indirect(offs_sb[:]))
+        words_picked = [keep.tile([P, S], U32, name="words_picked%d" % z, align_bytes=64) for z in range(PASSES)]
+        for z in range(PASSES):
+            nc.vector.tensor_copy(words_picked[z][:], words_all[z][:].indirect(offs_sb[:]))
+
+        w_grouped = keep.tile([P, PASSES, N, PACK], BF16, name="w_grouped", align_bytes=64)
+        for z in range(PASSES):
+            nc.scalar.copy(
+                w_grouped[:, z].rearrange("p (c i) j -> p c j i", i=4),
+                w_raw[:, z].rearrange("p j (c i) -> p c j i", i=4),
+            )
+        w_codes = keep.tile([P, PASSES * N], U32, name="w_codes", align_bytes=64)
+        w_scales = keep.tile([P, PASSES * N], U8, name="w_scales", align_bytes=64)
+        nc.vector.quantize_mx(
+            out=w_codes[:].bitcast(FP8X4),
+            scales=w_scales[:],
+            in_=w_grouped[:].rearrange("p z m j -> p (z m j)"),
+        )
+
+        banks = [psum.tile([P, BANK], F32, name="bank%d" % h) for h in range(halves)]
+        for z in range(PASSES):
+            for h in range(halves):
+                cols = slice(h * BANK, (h + 1) * BANK)
+                nc.tensor.matmul_mx(
+                    out=banks[h][:],
+                    lhsT=w_codes[:, z * N : (z + 1) * N].bitcast(FP8X4),
+                    lhsT_scale=w_scales[:, z * N : (z + 1) * N],
+                    rhs=words_picked[z][:, cols].bitcast(FP8X4),
+                    rhs_scale=scales_picked[4 * z : P, cols],
+                    start=(z == 0),
+                    stop=(z == PASSES - 1),
+                )
+
+        old = keep.tile([P, S], F32, name="old")
+        new = keep.tile([P, S], F32, name="new")
+        per = BANK // LANES
+        for h in range(halves):
+            nc.vector.tensor_copy(
+                old[:, h * BANK : (h + 1) * BANK],
+                store[:].indirect(slot_sb[:, h * per : (h + 1) * per]),
+            )
+        for h in range(halves):
+            cols = slice(h * BANK, (h + 1) * BANK)
+            nc.vector.tensor_tensor(new[:, cols], banks[h][:], old[:, cols], mybir.AluOpType.max)
+        nc.vector.tensor_copy(store[:].indirect(slot_sb[:]), new[:])
+        nc.sync.dma_start(out=out, in_=store[:])

@@ -29,34 +29,44 @@ def tile_picked_idxput_max_p_kernel(tc, x_words, x_scales, mem, w1, offs, slot, 
 
         offs_sb = keep.tile([P, S // LANES], U16, name="offs_sb")
         slot_sb = keep.tile([P, S // LANES], U16, name="slot_sb")
-        scales_all = keep.tile([P, T], U8, name="scales_all", align_bytes=64)
+        scales_all = keep.tile([P, T], U8, name="scales_all", tag="shared", align_bytes=64)
         words_all = [keep.tile([P, T], U32, name="words_all%d" % z, align_bytes=64) for z in range(PASSES)]
         w_raw = keep.tile([P, PASSES, PACK, N], F32, name="w_raw", align_bytes=64)
-        store = keep.tile([P, U], F32, name="store", align_bytes=64)
 
-        nc.vector.memset(scales_all[:].bitcast(I32), 0)
+        planes = keep.tile([P, PASSES * S], U8, name="planes", align_bytes=64)
+        nc.gpsimd.memset(scales_all[32:64, :].bitcast(I32), 0)
+        nc.vector.memset(scales_all[64:P, :].bitcast(I32), 0)
+        nc.vector.memset(planes[:].bitcast(I32), 0)
+        x_rows = x_words.rearrange("z p n t -> z p (n t)").bitcast(I32)
         nc.sync.dma_start(offs_sb[:], offs)
-        for q in range(4):
-            nc.sync.dma_start(
-                out=scales_all[32 * q : 32 * q + 4 * PASSES, :].bitcast(I32),
-                in_=x_scales[:, 4 * q : 4 * q + 4, :].bitcast(I32),
-            )
-        for z in range(PASSES):
-            nc.sync.dma_start(
-                out=words_all[z][:].bitcast(I32),
-                in_=x_words[z].rearrange("p n t -> p (n t)").bitcast(I32),
-            )
+        nc.sync.dma_start(
+            out=scales_all[0:32, :].bitcast(I32),
+            in_=x_scales.rearrange("z q n -> (z q) n").bitcast(I32),
+        )
+        nc.sync.dma_start(out=words_all[0][:].bitcast(I32), in_=x_rows[0])
         nc.sync.dma_start(out=w_raw[:], in_=w1.rearrange("(z p j) m -> p z j m", z=PASSES, j=PACK))
+        nc.sync.dma_start(out=words_all[1][:].bitcast(I32), in_=x_rows[1])
         nc.sync.dma_start(slot_sb[:], slot)
-        nc.sync.dma_start(out=store[:], in_=mem)
 
         scales_picked = keep.tile([P, S], U8, name="scales_picked", align_bytes=64)
         nc.vector.tensor_copy(scales_picked[:], scales_all[:].indirect(offs_sb[:]))
-        words_picked = [keep.tile([P, S], U32, name="words_picked%d" % z, align_bytes=64) for z in range(PASSES)]
-        for z in range(PASSES):
-            nc.vector.tensor_copy(words_picked[z][:], words_all[z][:].indirect(offs_sb[:]))
 
-        w_grouped = keep.tile([P, PASSES, N, PACK], BF16, name="w_grouped", align_bytes=64)
+        def place(z):
+            for q in range(4):
+                src = 16 * z + 4 * q
+                nc.sync.dma_start(
+                    out=planes[32 * q : 32 * q + 4, z * S : (z + 1) * S].bitcast(I32),
+                    in_=scales_picked[src : src + 4, :].bitcast(I32),
+                )
+
+        place(0)
+        store = keep.tile([P, U], F32, name="store", tag="shared", align_bytes=64)
+        nc.sync.dma_start(out=store[:], in_=mem)
+        place(1)
+        words_picked = [keep.tile([P, S], U32, name="words_picked0", align_bytes=64)]
+        nc.vector.tensor_copy(words_picked[0][:], words_all[0][:].indirect(offs_sb[:]))
+
+        w_grouped = keep.tile([P, PASSES, N, PACK], BF16, name="w_grouped", tag="staged", align_bytes=64)
         for z in range(PASSES):
             nc.scalar.copy(
                 w_grouped[:, z].rearrange("p (c i) j -> p c j i", i=4),
@@ -70,6 +80,9 @@ def tile_picked_idxput_max_p_kernel(tc, x_words, x_scales, mem, w1, offs, slot, 
             in_=w_grouped[:].rearrange("p z m j -> p (z m j)"),
         )
 
+        words_picked.append(keep.tile([P, S], U32, name="words_picked1", tag="staged", align_bytes=64))
+        nc.vector.tensor_copy(words_picked[1][:], words_all[1][:].indirect(offs_sb[:]))
+
         banks = [psum.tile([P, BANK], F32, name="bank%d" % h) for h in range(halves)]
         for z in range(PASSES):
             for h in range(halves):
@@ -79,7 +92,7 @@ def tile_picked_idxput_max_p_kernel(tc, x_words, x_scales, mem, w1, offs, slot, 
                     lhsT=w_codes[:, z * N : (z + 1) * N].bitcast(FP8X4),
                     lhsT_scale=w_scales[:, z * N : (z + 1) * N],
                     rhs=words_picked[z][:, cols].bitcast(FP8X4),
-                    rhs_scale=scales_picked[4 * z : P, cols],
+                    rhs_scale=planes[:, z * S + h * BANK : z * S + (h + 1) * BANK],
                     start=(z == 0),
                     stop=(z == PASSES - 1),
                 )

@@ -16,13 +16,18 @@ FP8X4 = mybir.dt.float8_e4m3fn_x4
 P = 128
 PACK = 4
 PASSES = K // (P * PACK)
-BANK = 512
 LANES = 16
+QUAD = 32
+ROWS = 4
+PLANE_ROW = (12, 0)
+WORD_CUTS = (0, 256, 512, 768, 1024)
+PIECE = 256
+MEM_CUTS = (0, 256, 512, 768, 1024)
+PUT_CUTS = (0, 512, 1024)
 
 
 def tile_picked_idxput_max_p_kernel(tc, x_words, x_scales, mem, w1, offs, slot, out):
     nc = tc.nc
-    halves = S // BANK
     with ExitStack() as ctx:
         keep = ctx.enter_context(tc.tile_pool(name="keep", bufs=1))
         psum = ctx.enter_context(tc.psum_pool(name="psum", bufs=1))
@@ -31,9 +36,9 @@ def tile_picked_idxput_max_p_kernel(tc, x_words, x_scales, mem, w1, offs, slot, 
         slot_sb = keep.tile([P, S // LANES], U16, name="slot_sb")
         scales_all = keep.tile([P, T], U8, name="scales_all", tag="shared", align_bytes=64)
         words_all = [keep.tile([P, T], U32, name="words_all%d" % z, align_bytes=64) for z in range(PASSES)]
-        w_raw = keep.tile([P, PASSES, PACK, N], F32, name="w_raw", align_bytes=64)
+        w_raw = keep.tile([P, PASSES, PACK, N], F32, name="w_raw", tag="staged", align_bytes=64)
 
-        planes = keep.tile([P, PASSES * S], U8, name="planes", align_bytes=64)
+        planes = keep.tile([P, S], U8, name="planes", align_bytes=64)
         nc.gpsimd.memset(scales_all[32:64, :].bitcast(I32), 0)
         nc.vector.memset(scales_all[64:P, :].bitcast(I32), 0)
         nc.vector.memset(planes[:].bitcast(I32), 0)
@@ -48,25 +53,28 @@ def tile_picked_idxput_max_p_kernel(tc, x_words, x_scales, mem, w1, offs, slot, 
         nc.sync.dma_start(out=words_all[1][:].bitcast(I32), in_=x_rows[1])
         nc.sync.dma_start(slot_sb[:], slot)
 
-        scales_picked = keep.tile([P, S], U8, name="scales_picked", align_bytes=64)
+        scales_picked = keep.tile([P, S], U8, name="scales_picked", tag="late", align_bytes=64)
         nc.vector.tensor_copy(scales_picked[:], scales_all[:].indirect(offs_sb[:]))
 
-        def place(z):
-            for q in range(4):
-                src = 16 * z + 4 * q
-                nc.sync.dma_start(
-                    out=planes[32 * q : 32 * q + 4, z * S : (z + 1) * S].bitcast(I32),
-                    in_=scales_picked[src : src + 4, :].bitcast(I32),
-                )
+        def move(dst, src, rows):
+            nc.sync.dma_start(
+                out=planes[dst : dst + rows, :].bitcast(I32),
+                in_=scales_picked[src : src + rows, :].bitcast(I32),
+            )
 
-        place(0)
+        move(PLANE_ROW[1], 16, ROWS)
+        for q in range(3):
+            move(QUAD * q + PLANE_ROW[0], ROWS * q, QUAD)
+        move(QUAD * 3 + PLANE_ROW[0], ROWS * 3, ROWS)
         store = keep.tile([P, U], F32, name="store", tag="shared", align_bytes=64)
         nc.sync.dma_start(out=store[:], in_=mem)
-        place(1)
+        result = keep.tile([P, U], F32, name="result", tag="late", align_bytes=64)
+        nc.sync.dma_start(out=result[:], in_=mem)
+
         words_picked = [keep.tile([P, S], U32, name="words_picked0", align_bytes=64)]
         nc.vector.tensor_copy(words_picked[0][:], words_all[0][:].indirect(offs_sb[:]))
 
-        w_grouped = keep.tile([P, PASSES, N, PACK], BF16, name="w_grouped", tag="staged", align_bytes=64)
+        w_grouped = keep.tile([P, PASSES, N, PACK], BF16, name="w_grouped", align_bytes=64)
         for z in range(PASSES):
             nc.scalar.copy(
                 w_grouped[:, z].rearrange("p (c i) j -> p c j i", i=4),
@@ -81,32 +89,37 @@ def tile_picked_idxput_max_p_kernel(tc, x_words, x_scales, mem, w1, offs, slot, 
         )
 
         words_picked.append(keep.tile([P, S], U32, name="words_picked1", tag="staged", align_bytes=64))
-        nc.vector.tensor_copy(words_picked[1][:], words_all[1][:].indirect(offs_sb[:]))
+        for a, b in zip(WORD_CUTS, WORD_CUTS[1:]):
+            nc.vector.tensor_copy(
+                words_picked[1][:, a:b], words_all[1][:].indirect(offs_sb[:, a // LANES : b // LANES])
+            )
 
-        banks = [psum.tile([P, BANK], F32, name="bank%d" % h) for h in range(halves)]
-        for z in range(PASSES):
-            for h in range(halves):
-                cols = slice(h * BANK, (h + 1) * BANK)
+        y = keep.tile([P, S], F32, name="y")
+        for h in range(S // PIECE):
+            cols = slice(h * PIECE, (h + 1) * PIECE)
+            bank = psum.tile([P, PIECE], F32, name="bank%d" % h)
+            for z in range(PASSES):
                 nc.tensor.matmul_mx(
-                    out=banks[h][:],
+                    out=bank[:],
                     lhsT=w_codes[:, z * N : (z + 1) * N].bitcast(FP8X4),
                     lhsT_scale=w_scales[:, z * N : (z + 1) * N],
                     rhs=words_picked[z][:, cols].bitcast(FP8X4),
-                    rhs_scale=planes[:, z * S + h * BANK : z * S + (h + 1) * BANK],
+                    rhs_scale=planes[PLANE_ROW[z] : P, cols],
                     start=(z == 0),
                     stop=(z == PASSES - 1),
                 )
+            nc.scalar.copy(y[:, cols], bank[:])
 
-        old = keep.tile([P, S], F32, name="old")
-        new = keep.tile([P, S], F32, name="new")
-        per = BANK // LANES
-        for h in range(halves):
-            nc.vector.tensor_copy(
-                old[:, h * BANK : (h + 1) * BANK],
-                store[:].indirect(slot_sb[:, h * per : (h + 1) * per]),
+        gap = keep.tile([P, S], F32, name="gap")
+        lift = keep.tile([P, S], F32, name="lift", tag="staged", align_bytes=64)
+        for a, b in zip(MEM_CUTS, MEM_CUTS[1:]):
+            nc.vector.tensor_tensor(
+                gap[:, a:b], store[:].indirect(slot_sb[:, a // LANES : b // LANES]), y[:, a:b], mybir.AluOpType.subtract
             )
-        for h in range(halves):
-            cols = slice(h * BANK, (h + 1) * BANK)
-            nc.vector.tensor_tensor(new[:, cols], banks[h][:], old[:, cols], mybir.AluOpType.max)
-        nc.vector.tensor_copy(store[:].indirect(slot_sb[:]), new[:])
-        nc.sync.dma_start(out=out, in_=store[:])
+        for a, b in zip(PUT_CUTS, PUT_CUTS[1:]):
+            nc.scalar.activation(lift[:, a:b], gap[:, a:b], mybir.ActivationFunctionType.Relu)
+        for a, b in zip(PUT_CUTS, PUT_CUTS[1:]):
+            nc.vector.tensor_tensor(
+                result[:].indirect(slot_sb[:, a // LANES : b // LANES]), y[:, a:b], lift[:, a:b], mybir.AluOpType.add
+            )
+        nc.sync.dma_start(out=out, in_=result[:])

@@ -19,10 +19,9 @@ PASSES = K // (P * PACK)
 LANES = 16
 QUAD = 32
 ROWS = 4
-PLANE_ROW = (12, 0)
-WORD_CUTS = (0, 256, 512, 768, 1024)
+PLANE_ROW = (0, 4)
 PIECE = 256
-MEM_CUTS = (0, 256, 512, 768, 1024)
+MEM_CUTS = (0, 256, 512, 1024)
 PUT_CUTS = (0, 512, 1024)
 
 
@@ -36,36 +35,31 @@ def tile_picked_idxput_max_p_kernel(tc, x_words, x_scales, mem, w1, offs, slot, 
         slot_sb = keep.tile([P, S // LANES], U16, name="slot_sb")
         scales_all = keep.tile([P, T], U8, name="scales_all", tag="shared", align_bytes=64)
         words_all = [keep.tile([P, T], U32, name="words_all%d" % z, align_bytes=64) for z in range(PASSES)]
-        w_raw = keep.tile([P, PASSES, PACK, N], F32, name="w_raw", tag="staged", align_bytes=64)
+        w_raw = [keep.tile([P, PACK, N], F32, name="w_raw%d" % z, tag="staged%d" % z, align_bytes=64) for z in range(PASSES)]
 
         planes = keep.tile([P, S], U8, name="planes", align_bytes=64)
         nc.gpsimd.memset(scales_all[32:64, :].bitcast(I32), 0)
         nc.vector.memset(scales_all[64:P, :].bitcast(I32), 0)
-        nc.vector.memset(planes[:].bitcast(I32), 0)
         x_rows = x_words.rearrange("z p n t -> z p (n t)").bitcast(I32)
         nc.sync.dma_start(offs_sb[:], offs)
         nc.sync.dma_start(
             out=scales_all[0:32, :].bitcast(I32),
-            in_=x_scales.rearrange("z q n -> (z q) n").bitcast(I32),
+            in_=x_scales.bitcast(I32).rearrange("z r n -> r z n"),
         )
-        nc.sync.dma_start(out=words_all[0][:].bitcast(I32), in_=x_rows[0])
-        nc.sync.dma_start(out=w_raw[:], in_=w1.rearrange("(z p j) m -> p z j m", z=PASSES, j=PACK))
-        nc.sync.dma_start(out=words_all[1][:].bitcast(I32), in_=x_rows[1])
+        w_rows = w1.rearrange("(z p j) m -> z p j m", z=PASSES, j=PACK)
+        for z in range(PASSES):
+            nc.sync.dma_start(out=words_all[z][:].bitcast(I32), in_=x_rows[z])
+            nc.sync.dma_start(out=w_raw[z][:], in_=w_rows[z])
         nc.sync.dma_start(slot_sb[:], slot)
 
         scales_picked = keep.tile([P, S], U8, name="scales_picked", tag="late", align_bytes=64)
         nc.vector.tensor_copy(scales_picked[:], scales_all[:].indirect(offs_sb[:]))
 
-        def move(dst, src, rows):
+        for j in range(ROWS):
             nc.sync.dma_start(
-                out=planes[dst : dst + rows, :].bitcast(I32),
-                in_=scales_picked[src : src + rows, :].bitcast(I32),
+                out=planes[j:P:ROWS, :].bitcast(I32),
+                in_=scales_picked[PASSES * j : PASSES * j + QUAD, :].bitcast(I32),
             )
-
-        move(PLANE_ROW[1], 16, ROWS)
-        for q in range(3):
-            move(QUAD * q + PLANE_ROW[0], ROWS * q, QUAD)
-        move(QUAD * 3 + PLANE_ROW[0], ROWS * 3, ROWS)
         store = keep.tile([P, U], F32, name="store", tag="shared", align_bytes=64)
         nc.sync.dma_start(out=store[:], in_=mem)
         result = keep.tile([P, U], F32, name="result", tag="late", align_bytes=64)
@@ -74,25 +68,37 @@ def tile_picked_idxput_max_p_kernel(tc, x_words, x_scales, mem, w1, offs, slot, 
         words_picked = [keep.tile([P, S], U32, name="words_picked0", align_bytes=64)]
         nc.vector.tensor_copy(words_picked[0][:], words_all[0][:].indirect(offs_sb[:]))
 
-        w_grouped = keep.tile([P, PASSES, N, PACK], BF16, name="w_grouped", align_bytes=64)
-        for z in range(PASSES):
-            nc.scalar.copy(
-                w_grouped[:, z].rearrange("p (c i) j -> p c j i", i=4),
-                w_raw[:, z].rearrange("p j (c i) -> p c j i", i=4),
-            )
         w_codes = keep.tile([P, PASSES * N], U32, name="w_codes", align_bytes=64)
         w_scales = keep.tile([P, PASSES * N], U8, name="w_scales", align_bytes=64)
-        nc.vector.quantize_mx(
-            out=w_codes[:].bitcast(FP8X4),
-            scales=w_scales[:],
-            in_=w_grouped[:].rearrange("p z m j -> p (z m j)"),
-        )
 
-        words_picked.append(keep.tile([P, S], U32, name="words_picked1", tag="staged", align_bytes=64))
-        for a, b in zip(WORD_CUTS, WORD_CUTS[1:]):
-            nc.vector.tensor_copy(
-                words_picked[1][:, a:b], words_all[1][:].indirect(offs_sb[:, a // LANES : b // LANES])
+        def quantise(z):
+            w_grouped = keep.tile([P, N, PACK], BF16, name="w_grouped%d" % z, align_bytes=64)
+            nc.scalar.copy(
+                w_grouped[:].rearrange("p (c i) j -> p c j i", i=4),
+                w_raw[z][:].rearrange("p j (c i) -> p c j i", i=4),
             )
+            nc.vector.quantize_mx(
+                out=w_codes[:, z * N : (z + 1) * N].bitcast(FP8X4),
+                scales=w_scales[:, z * N : (z + 1) * N],
+                in_=w_grouped[:].rearrange("p m j -> p (m j)"),
+            )
+
+        second = []
+        for z in range(PASSES):
+            quantise(z)
+            half = keep.tile([P, S // 2], U32, name="words_picked1_%d" % z, tag="staged%d" % z, align_bytes=64)
+            second.append(half)
+            for c in range(2):
+                a = z * 512 + c * 256
+                nc.vector.tensor_copy(
+                    half[:, c * 256 : (c + 1) * 256],
+                    words_all[1][:].indirect(offs_sb[:, a // LANES : (a + 256) // LANES]),
+                )
+
+        def moving(z, h):
+            if z == 0:
+                return words_picked[0][:, h * PIECE : (h + 1) * PIECE]
+            return second[h // 2][:, (h % 2) * PIECE : (h % 2 + 1) * PIECE]
 
         y = keep.tile([P, S], F32, name="y")
         for h in range(S // PIECE):
@@ -103,7 +109,7 @@ def tile_picked_idxput_max_p_kernel(tc, x_words, x_scales, mem, w1, offs, slot, 
                     out=bank[:],
                     lhsT=w_codes[:, z * N : (z + 1) * N].bitcast(FP8X4),
                     lhsT_scale=w_scales[:, z * N : (z + 1) * N],
-                    rhs=words_picked[z][:, cols].bitcast(FP8X4),
+                    rhs=moving(z, h).bitcast(FP8X4),
                     rhs_scale=planes[PLANE_ROW[z] : P, cols],
                     start=(z == 0),
                     stop=(z == PASSES - 1),
@@ -111,7 +117,7 @@ def tile_picked_idxput_max_p_kernel(tc, x_words, x_scales, mem, w1, offs, slot, 
             nc.scalar.copy(y[:, cols], bank[:])
 
         gap = keep.tile([P, S], F32, name="gap")
-        lift = keep.tile([P, S], F32, name="lift", tag="staged", align_bytes=64)
+        lift = keep.tile([P, S], F32, name="lift", tag="staged1", align_bytes=64)
         for a, b in zip(MEM_CUTS, MEM_CUTS[1:]):
             nc.vector.tensor_tensor(
                 gap[:, a:b], store[:].indirect(slot_sb[:, a // LANES : b // LANES]), y[:, a:b], mybir.AluOpType.subtract
@@ -122,4 +128,5 @@ def tile_picked_idxput_max_p_kernel(tc, x_words, x_scales, mem, w1, offs, slot, 
             nc.vector.tensor_tensor(
                 result[:].indirect(slot_sb[:, a // LANES : b // LANES]), y[:, a:b], lift[:, a:b], mybir.AluOpType.add
             )
-        nc.sync.dma_start(out=out, in_=result[:])
+        for c in range(0, U, U // 2):
+            nc.sync.dma_start(out=out[:, c : c + U // 2], in_=result[:, c : c + U // 2])

@@ -21,7 +21,7 @@ QUAD = 32
 ROWS = 4
 PLANE_ROW = (0, 4)
 PIECE = 256
-MEM_CUTS = (0, 256, 512, 1024)
+MEM_CUTS = (0, 512, 1024)
 PUT_CUTS = (0, 512, 1024)
 
 
@@ -88,12 +88,8 @@ def tile_picked_idxput_max_p_kernel(tc, x_words, x_scales, mem, w1, offs, slot, 
             quantise(z)
             half = keep.tile([P, S // 2], U32, name="words_picked1_%d" % z, tag="staged%d" % z, align_bytes=64)
             second.append(half)
-            for c in range(2):
-                a = z * 512 + c * 256
-                nc.vector.tensor_copy(
-                    half[:, c * 256 : (c + 1) * 256],
-                    words_all[1][:].indirect(offs_sb[:, a // LANES : (a + 256) // LANES]),
-                )
+            a = z * 512
+            nc.vector.tensor_copy(half[:], words_all[1][:].indirect(offs_sb[:, a // LANES : (a + 512) // LANES]))
 
         def moving(z, h):
             if z == 0:
@@ -101,20 +97,22 @@ def tile_picked_idxput_max_p_kernel(tc, x_words, x_scales, mem, w1, offs, slot, 
             return second[h // 2][:, (h % 2) * PIECE : (h % 2 + 1) * PIECE]
 
         y = keep.tile([P, S], F32, name="y")
-        for h in range(S // PIECE):
-            cols = slice(h * PIECE, (h + 1) * PIECE)
-            bank = psum.tile([P, PIECE], F32, name="bank%d" % h)
+        banks = [psum.tile([P, PIECE], F32, name="bank%d" % h) for h in range(S // PIECE)]
+        for pair in range(2):
             for z in range(PASSES):
-                nc.tensor.matmul_mx(
-                    out=bank[:],
-                    lhsT=w_codes[:, z * N : (z + 1) * N].bitcast(FP8X4),
-                    lhsT_scale=w_scales[:, z * N : (z + 1) * N],
-                    rhs=moving(z, h).bitcast(FP8X4),
-                    rhs_scale=planes[PLANE_ROW[z] : P, cols],
-                    start=(z == 0),
-                    stop=(z == PASSES - 1),
-                )
-            nc.scalar.copy(y[:, cols], bank[:])
+                for h in (2 * pair, 2 * pair + 1):
+                    cols = slice(h * PIECE, (h + 1) * PIECE)
+                    nc.tensor.matmul_mx(
+                        out=banks[h][:],
+                        lhsT=w_codes[:, z * N : (z + 1) * N].bitcast(FP8X4),
+                        lhsT_scale=w_scales[:, z * N : (z + 1) * N],
+                        rhs=moving(z, h).bitcast(FP8X4),
+                        rhs_scale=planes[PLANE_ROW[z] : P, cols],
+                        start=(z == 0),
+                        stop=(z == PASSES - 1),
+                    )
+                    if z == PASSES - 1:
+                        nc.scalar.copy(y[:, cols], banks[h][:])
 
         gap = keep.tile([P, S], F32, name="gap")
         lift = keep.tile([P, S], F32, name="lift", tag="staged1", align_bytes=64)

@@ -38,12 +38,12 @@ def tile_picked_idxput_max_p_kernel(tc, x_words, x_scales, mem, w1, offs, slot, 
         w_raw = [keep.tile([P, PACK, N], F32, name="w_raw%d" % z, tag="staged%d" % z, align_bytes=64) for z in range(PASSES)]
 
         planes = keep.tile([P, S], U8, name="planes", align_bytes=64)
-        nc.gpsimd.memset(scales_all[32:64, :].bitcast(I32), 0)
-        nc.vector.memset(scales_all[64:P, :].bitcast(I32), 0)
+        nc.vector.memset(scales_all[0:64, :].bitcast(I32), 0)
+        nc.vector.memset(scales_all[96:P, :].bitcast(I32), 0)
         x_rows = x_words.rearrange("z p n t -> z p (n t)").bitcast(I32)
         nc.sync.dma_start(offs_sb[:], offs)
         nc.sync.dma_start(
-            out=scales_all[0:32, :].bitcast(I32),
+            out=scales_all[64:96, :].bitcast(I32),
             in_=x_scales.bitcast(I32).rearrange("z r n -> r z n"),
         )
         w_rows = w1.rearrange("(z p j) m -> z p j m", z=PASSES, j=PACK)
@@ -58,7 +58,7 @@ def tile_picked_idxput_max_p_kernel(tc, x_words, x_scales, mem, w1, offs, slot, 
         for j in range(ROWS):
             nc.sync.dma_start(
                 out=planes[j:P:ROWS, :].bitcast(I32),
-                in_=scales_picked[PASSES * j : PASSES * j + QUAD, :].bitcast(I32),
+                in_=scales_picked[64 + PASSES * j : 64 + PASSES * j + QUAD, :].bitcast(I32),
             )
         store = keep.tile([P, U], F32, name="store", tag="shared", align_bytes=64)
         nc.sync.dma_start(out=store[:], in_=mem)

@@ -41,11 +41,11 @@ def tile_picked_idxput_max_p_kernel(tc, x_words, x_scales, mem, w1, offs, slot, 
         nc.vector.memset(scales_all[0:64, :].bitcast(I32), 0)
         nc.vector.memset(scales_all[96:P, :].bitcast(I32), 0)
         x_rows = x_words.rearrange("z p n t -> z p (n t)").bitcast(I32)
-        nc.sync.dma_start(offs_sb[:], offs)
         nc.sync.dma_start(
             out=scales_all[64:96, :].bitcast(I32),
             in_=x_scales.bitcast(I32).rearrange("z r n -> r z n"),
         )
+        nc.sync.dma_start(offs_sb[:], offs)
         w_rows = w1.rearrange("(z p j) m -> z p j m", z=PASSES, j=PACK)
         for z in range(PASSES):
             nc.sync.dma_start(out=words_all[z][:].bitcast(I32), in_=x_rows[z])

@@ -29,11 +29,12 @@ def tile_picked_idxput_max_p_kernel(tc, x_words, x_scales, mem, w1, offs, slot, 
     nc = tc.nc
     with ExitStack() as ctx:
         keep = ctx.enter_context(tc.tile_pool(name="keep", bufs=1))
+        windows = ctx.enter_context(tc.tile_pool(name="windows", bufs=1))
         psum = ctx.enter_context(tc.psum_pool(name="psum", bufs=1))
 
         offs_sb = keep.tile([P, S // LANES], U16, name="offs_sb")
         slot_sb = keep.tile([P, S // LANES], U16, name="slot_sb")
-        scales_all = keep.tile([P, T], U8, name="scales_all", tag="shared", align_bytes=64)
+        scales_all = windows.tile([P, T], U8, name="scales_all", offset=4 * U - T // 2, align_bytes=64)
         words_all = [keep.tile([P, T], U32, name="words_all%d" % z, align_bytes=64) for z in range(PASSES)]
         w_raw = [keep.tile([P, PACK, N], F32, name="w_raw%d" % z, tag="staged%d" % z, align_bytes=64) for z in range(PASSES)]
 
@@ -52,7 +53,7 @@ def tile_picked_idxput_max_p_kernel(tc, x_words, x_scales, mem, w1, offs, slot, 
             nc.sync.dma_start(out=w_raw[z][:], in_=w_rows[z])
         nc.sync.dma_start(slot_sb[:], slot)
 
-        scales_picked = keep.tile([P, S], U8, name="scales_picked", tag="late", align_bytes=64)
+        scales_picked = keep.tile([P, S], U8, name="scales_picked", align_bytes=64)
         nc.vector.tensor_copy(scales_picked[:], scales_all[:].indirect(offs_sb[:]))
 
         for j in range(ROWS):
@@ -60,9 +61,9 @@ def tile_picked_idxput_max_p_kernel(tc, x_words, x_scales, mem, w1, offs, slot, 
                 out=planes[j:P:ROWS, :].bitcast(I32),
                 in_=scales_picked[64 + PASSES * j : 64 + PASSES * j + QUAD, :].bitcast(I32),
             )
-        store = keep.tile([P, U], F32, name="store", tag="shared", align_bytes=64)
+        store = windows.tile([P, U], F32, name="store", offset=0, align_bytes=64)
         nc.sync.dma_start(out=store[:], in_=mem)
-        result = keep.tile([P, U], F32, name="result", tag="late", align_bytes=64)
+        result = windows.tile([P, U], F32, name="result", offset=4 * U, align_bytes=64)
         nc.sync.dma_start(out=result[:], in_=mem)
 
         words_picked = [keep.tile([P, S], U32, name="words_picked0", align_bytes=64)]

@@ -127,5 +127,5 @@ def tile_picked_idxput_max_p_kernel(tc, x_words, x_scales, mem, w1, offs, slot, 
             nc.vector.tensor_tensor(
                 result[:].indirect(slot_sb[:, a // LANES : b // LANES]), y[:, a:b], lift[:, a:b], mybir.AluOpType.add
             )
-        for c in range(0, U, U // 2):
-            nc.sync.dma_start(out=out[:, c : c + U // 2], in_=result[:, c : c + U // 2])
+        for e in range(2):
+            nc.sync.dma_start(out=out[e:P:2, :], in_=result[e:P:2, :])

@@ -12,6 +12,8 @@ U32 = mybir.dt.uint32
 U16 = mybir.dt.uint16
 U8 = mybir.dt.uint8
 FP8X4 = mybir.dt.float8_e4m3fn_x4
+COPY = mybir.ActivationFunctionType.Copy
+MAX = mybir.AluOpType.max
 
 P = 128
 PACK = 4
@@ -20,9 +22,12 @@ LANES = 16
 QUAD = 32
 ROWS = 4
 PLANE_ROW = (0, 4)
+HALF = S // 2
 PIECE = 256
-MEM_CUTS = (0, 512, 1024)
-PUT_CUTS = (0, 512, 1024)
+BANK_CUTS = (0, 256, 768, 1024)
+VECTOR_FETCH_CUTS = (0, 256, 448)
+VECTOR_PUT = (256, 736)
+STORE_CUTS = (0, 512, 1024, 1536, 2048)
 
 
 def tile_picked_idxput_max_p_kernel(tc, x_words, x_scales, mem, w1, offs, slot, out):
@@ -34,11 +39,14 @@ def tile_picked_idxput_max_p_kernel(tc, x_words, x_scales, mem, w1, offs, slot, 
 
         offs_sb = keep.tile([P, S // LANES], U16, name="offs_sb")
         slot_sb = keep.tile([P, S // LANES], U16, name="slot_sb")
+
+        def slots(a, b):
+            return slot_sb[:, a // LANES : b // LANES]
+
         scales_all = windows.tile([P, T], U8, name="scales_all", offset=4 * U - T // 2, align_bytes=64)
         words_all = [keep.tile([P, T], U32, name="words_all%d" % z, align_bytes=64) for z in range(PASSES)]
         w_raw = [keep.tile([P, PACK, N], F32, name="w_raw%d" % z, tag="staged%d" % z, align_bytes=64) for z in range(PASSES)]
 
-        planes = keep.tile([P, S], U8, name="planes", align_bytes=64)
         nc.vector.memset(scales_all[0:64, :].bitcast(I32), 0)
         nc.vector.memset(scales_all[96:P, :].bitcast(I32), 0)
         x_rows = x_words.rearrange("z p n t -> z p (n t)").bitcast(I32)
@@ -56,23 +64,24 @@ def tile_picked_idxput_max_p_kernel(tc, x_words, x_scales, mem, w1, offs, slot, 
         scales_picked = keep.tile([P, S], U8, name="scales_picked", align_bytes=64)
         nc.vector.tensor_copy(scales_picked[:], scales_all[:].indirect(offs_sb[:]))
 
+        planes = keep.tile([P, S], U8, name="planes", align_bytes=64)
         for j in range(ROWS):
             nc.sync.dma_start(
                 out=planes[j:P:ROWS, :].bitcast(I32),
                 in_=scales_picked[64 + PASSES * j : 64 + PASSES * j + QUAD, :].bitcast(I32),
             )
-        store = windows.tile([P, U], F32, name="store", offset=0, align_bytes=64)
-        nc.sync.dma_start(out=store[:], in_=mem)
-        result = windows.tile([P, U], F32, name="result", offset=4 * U, align_bytes=64)
-        nc.sync.dma_start(out=result[:], in_=mem)
+        mem_scalar = windows.tile([P, U], F32, name="mem_scalar", offset=0, align_bytes=64)
+        nc.sync.dma_start(out=mem_scalar[:], in_=mem)
+        mem_vector = windows.tile([P, U], F32, name="mem_vector", offset=4 * U, align_bytes=64)
+        nc.sync.dma_start(out=mem_vector[:], in_=mem)
 
-        words_picked = [keep.tile([P, S], U32, name="words_picked0", align_bytes=64)]
-        nc.vector.tensor_copy(words_picked[0][:], words_all[0][:].indirect(offs_sb[:]))
+        first = keep.tile([P, S], U32, name="words_picked0", align_bytes=64)
+        nc.vector.tensor_copy(first[:], words_all[0][:].indirect(offs_sb[:]))
 
         w_codes = keep.tile([P, PASSES * N], U32, name="w_codes", align_bytes=64)
         w_scales = keep.tile([P, PASSES * N], U8, name="w_scales", align_bytes=64)
-
-        def quantise(z):
+        second = []
+        for z in range(PASSES):
             w_grouped = keep.tile([P, N, PACK], BF16, name="w_grouped%d" % z, align_bytes=64)
             nc.scalar.copy(
                 w_grouped[:].rearrange("p (c i) j -> p c j i", i=4),
@@ -83,49 +92,44 @@ def tile_picked_idxput_max_p_kernel(tc, x_words, x_scales, mem, w1, offs, slot, 
                 scales=w_scales[:, z * N : (z + 1) * N],
                 in_=w_grouped[:].rearrange("p m j -> p (m j)"),
             )
-
-        second = []
-        for z in range(PASSES):
-            quantise(z)
-            half = keep.tile([P, S // 2], U32, name="words_picked1_%d" % z, tag="staged%d" % z, align_bytes=64)
+            half = keep.tile([P, HALF], U32, name="words_picked1_%d" % z, tag="staged%d" % z, align_bytes=64)
             second.append(half)
-            a = z * 512
-            nc.vector.tensor_copy(half[:], words_all[1][:].indirect(offs_sb[:, a // LANES : (a + 512) // LANES]))
+            a = z * HALF
+            nc.vector.tensor_copy(half[:], words_all[1][:].indirect(offs_sb[:, a // LANES : (a + HALF) // LANES]))
 
-        def moving(z, h):
+        def moving(z, a, b):
             if z == 0:
-                return words_picked[0][:, h * PIECE : (h + 1) * PIECE]
-            return second[h // 2][:, (h % 2) * PIECE : (h % 2 + 1) * PIECE]
+                return first[:, a:b]
+            return second[a // HALF][:, a % HALF : a % HALF + b - a]
 
-        y = keep.tile([P, S], F32, name="y")
-        banks = [psum.tile([P, PIECE], F32, name="bank%d" % h) for h in range(S // PIECE)]
-        for pair in range(2):
-            for z in range(PASSES):
-                for h in (2 * pair, 2 * pair + 1):
-                    cols = slice(h * PIECE, (h + 1) * PIECE)
+        old = keep.tile([P, S], F32, name="old")
+        for a, b in zip(VECTOR_FETCH_CUTS, VECTOR_FETCH_CUTS[1:]):
+            nc.vector.tensor_copy(old[:, a:b], mem_scalar[:].indirect(slots(a, b)))
+        a = VECTOR_FETCH_CUTS[-1]
+        nc.scalar.activation(old[:, a:S], mem_scalar[:].indirect(slots(a, S)), COPY)
+
+        new = keep.tile([P, S], F32, name="new")
+        for a, b in zip(BANK_CUTS, BANK_CUTS[1:]):
+            bank = psum.tile([P, b - a], F32, name="bank%d" % a)
+            for c in range(a, b, PIECE):
+                for z in range(PASSES):
                     nc.tensor.matmul_mx(
-                        out=banks[h][:],
+                        out=bank[:, c - a : c - a + PIECE],
                         lhsT=w_codes[:, z * N : (z + 1) * N].bitcast(FP8X4),
                         lhsT_scale=w_scales[:, z * N : (z + 1) * N],
-                        rhs=moving(z, h).bitcast(FP8X4),
-                        rhs_scale=planes[PLANE_ROW[z] : P, cols],
+                        rhs=moving(z, c, c + PIECE).bitcast(FP8X4),
+                        rhs_scale=planes[PLANE_ROW[z] : P, c : c + PIECE],
                         start=(z == 0),
                         stop=(z == PASSES - 1),
                     )
-                    if z == PASSES - 1:
-                        nc.scalar.copy(y[:, cols], banks[h][:])
+            nc.vector.tensor_tensor(new[:, a:b], bank[:], old[:, a:b], MAX)
 
-        gap = keep.tile([P, S], F32, name="gap")
-        lift = keep.tile([P, S], F32, name="lift", tag="staged1", align_bytes=64)
-        for a, b in zip(MEM_CUTS, MEM_CUTS[1:]):
-            nc.vector.tensor_tensor(
-                gap[:, a:b], store[:].indirect(slot_sb[:, a // LANES : b // LANES]), y[:, a:b], mybir.AluOpType.subtract
-            )
-        for a, b in zip(PUT_CUTS, PUT_CUTS[1:]):
-            nc.scalar.activation(lift[:, a:b], gap[:, a:b], mybir.ActivationFunctionType.Relu)
-        for a, b in zip(PUT_CUTS, PUT_CUTS[1:]):
-            nc.vector.tensor_tensor(
-                result[:].indirect(slot_sb[:, a // LANES : b // LANES]), y[:, a:b], lift[:, a:b], mybir.AluOpType.add
-            )
-        for e in range(2):
-            nc.sync.dma_start(out=out[e:P:2, :], in_=result[e:P:2, :])
+        a, b = VECTOR_PUT
+        nc.scalar.activation(mem_scalar[:].indirect(slots(0, a)), new[:, 0:a], COPY)
+        nc.scalar.activation(mem_scalar[:].indirect(slots(b, S)), new[:, b:S], COPY)
+        nc.vector.tensor_copy(mem_vector[:].indirect(slots(a, b)), new[:, a:b])
+
+        merged = keep.tile([P, U], F32, name="merged")
+        for a, b in zip(STORE_CUTS, STORE_CUTS[1:]):
+            nc.vector.tensor_tensor(merged[:, a:b], mem_scalar[:, a:b], mem_vector[:, a:b], MAX)
+            nc.sync.dma_start(out=out[:, a:b], in_=merged[:, a:b])

@@ -26,8 +26,9 @@ HALF = S // 2
 PIECE = 256
 BANK_CUTS = (0, 256, 768, 1024)
 VECTOR_FETCH_CUTS = (0, 256, 448)
+SCALAR_FETCH_CUTS = (448, 768, 1024)
 VECTOR_PUT = (256, 736)
-STORE_CUTS = (0, 512, 1024, 1536, 2048)
+STORE_CUTS = (0, 368, 832, 1392, 2048)
 
 
 def tile_picked_idxput_max_p_kernel(tc, x_words, x_scales, mem, w1, offs, slot, out):
@@ -45,7 +46,7 @@ def tile_picked_idxput_max_p_kernel(tc, x_words, x_scales, mem, w1, offs, slot, 
 
         scales_all = windows.tile([P, T], U8, name="scales_all", offset=4 * U - T // 2, align_bytes=64)
         words_all = [keep.tile([P, T], U32, name="words_all%d" % z, align_bytes=64) for z in range(PASSES)]
-        w_raw = [keep.tile([P, PACK, N], F32, name="w_raw%d" % z, tag="staged%d" % z, align_bytes=64) for z in range(PASSES)]
+        w_raw = keep.tile([P, PASSES, PACK, N], F32, name="w_raw", align_bytes=64)
 
         nc.vector.memset(scales_all[0:64, :].bitcast(I32), 0)
         nc.vector.memset(scales_all[96:P, :].bitcast(I32), 0)
@@ -55,10 +56,9 @@ def tile_picked_idxput_max_p_kernel(tc, x_words, x_scales, mem, w1, offs, slot, 
             in_=x_scales.bitcast(I32).rearrange("z r n -> r z n"),
         )
         nc.sync.dma_start(offs_sb[:], offs)
-        w_rows = w1.rearrange("(z p j) m -> z p j m", z=PASSES, j=PACK)
         for z in range(PASSES):
             nc.sync.dma_start(out=words_all[z][:].bitcast(I32), in_=x_rows[z])
-            nc.sync.dma_start(out=w_raw[z][:], in_=w_rows[z])
+        nc.sync.dma_start(out=w_raw[:], in_=w1.rearrange("(z p j) m -> p z j m", z=PASSES, j=PACK))
         nc.sync.dma_start(slot_sb[:], slot)
 
         scales_picked = keep.tile([P, S], U8, name="scales_picked", align_bytes=64)
@@ -82,46 +82,47 @@ def tile_picked_idxput_max_p_kernel(tc, x_words, x_scales, mem, w1, offs, slot, 
         w_scales = keep.tile([P, PASSES * N], U8, name="w_scales", align_bytes=64)
         second = []
         for z in range(PASSES):
-            w_grouped = keep.tile([P, N, PACK], BF16, name="w_grouped%d" % z, align_bytes=64)
+            half = keep.tile([P, HALF], U32, name="words_picked1_%d" % z, tag="staged%d" % z, align_bytes=64)
+            second.append(half)
+            a = z * HALF
+            nc.vector.tensor_copy(half[:], words_all[1][:].indirect(offs_sb[:, a // LANES : (a + HALF) // LANES]))
+            w_grouped = keep.tile([P, N, PACK], BF16, name="w_grouped%d" % z, tag="staged%d" % (z + 1), align_bytes=64)
             nc.scalar.copy(
                 w_grouped[:].rearrange("p (c i) j -> p c j i", i=4),
-                w_raw[z][:].rearrange("p j (c i) -> p c j i", i=4),
+                w_raw[:, z].rearrange("p j (c i) -> p c j i", i=4),
             )
             nc.vector.quantize_mx(
                 out=w_codes[:, z * N : (z + 1) * N].bitcast(FP8X4),
                 scales=w_scales[:, z * N : (z + 1) * N],
                 in_=w_grouped[:].rearrange("p m j -> p (m j)"),
             )
-            half = keep.tile([P, HALF], U32, name="words_picked1_%d" % z, tag="staged%d" % z, align_bytes=64)
-            second.append(half)
-            a = z * HALF
-            nc.vector.tensor_copy(half[:], words_all[1][:].indirect(offs_sb[:, a // LANES : (a + HALF) // LANES]))
-
-        def moving(z, a, b):
-            if z == 0:
-                return first[:, a:b]
-            return second[a // HALF][:, a % HALF : a % HALF + b - a]
 
         old = keep.tile([P, S], F32, name="old")
         for a, b in zip(VECTOR_FETCH_CUTS, VECTOR_FETCH_CUTS[1:]):
             nc.vector.tensor_copy(old[:, a:b], mem_scalar[:].indirect(slots(a, b)))
-        a = VECTOR_FETCH_CUTS[-1]
-        nc.scalar.activation(old[:, a:S], mem_scalar[:].indirect(slots(a, S)), COPY)
+        for a, b in zip(SCALAR_FETCH_CUTS, SCALAR_FETCH_CUTS[1:]):
+            nc.scalar.activation(old[:, a:b], mem_scalar[:].indirect(slots(a, b)), COPY)
 
         new = keep.tile([P, S], F32, name="new")
-        for a, b in zip(BANK_CUTS, BANK_CUTS[1:]):
-            bank = psum.tile([P, b - a], F32, name="bank%d" % a)
+        banks = [(a, b, psum.tile([P, b - a], F32, name="bank%d" % a)) for a, b in zip(BANK_CUTS, BANK_CUTS[1:])]
+
+        def product(z, codes, a, b, into, last):
+            nc.tensor.matmul_mx(
+                out=into,
+                lhsT=w_codes[:, z * N : (z + 1) * N].bitcast(FP8X4),
+                lhsT_scale=w_scales[:, z * N : (z + 1) * N],
+                rhs=codes.bitcast(FP8X4),
+                rhs_scale=planes[PLANE_ROW[z] : P, a:b],
+                start=(z == 0),
+                stop=last,
+            )
+
+        for a, b, bank in banks:
+            product(0, first[:, a:b], a, b, bank[:], False)
+        for a, b, bank in banks:
             for c in range(a, b, PIECE):
-                for z in range(PASSES):
-                    nc.tensor.matmul_mx(
-                        out=bank[:, c - a : c - a + PIECE],
-                        lhsT=w_codes[:, z * N : (z + 1) * N].bitcast(FP8X4),
-                        lhsT_scale=w_scales[:, z * N : (z + 1) * N],
-                        rhs=moving(z, c, c + PIECE).bitcast(FP8X4),
-                        rhs_scale=planes[PLANE_ROW[z] : P, c : c + PIECE],
-                        start=(z == 0),
-                        stop=(z == PASSES - 1),
-                    )
+                codes = second[c // HALF][:, c % HALF : c % HALF + PIECE]
+                product(1, codes, c, c + PIECE, bank[:, c - a : c - a + PIECE], c + PIECE == b)
             nc.vector.tensor_tensor(new[:, a:b], bank[:], old[:, a:b], MAX)
 
         a, b = VECTOR_PUT

@@ -22,12 +22,13 @@ LANES = 16
 QUAD = 32
 ROWS = 4
 PLANE_ROW = (0, 4)
-HALF = S // 2
-PIECE = 256
+WORD_CUT = 640
+PRODUCT_CUTS = (0, 256, 512, 640, 768, 1024)
 BANK_CUTS = (0, 256, 768, 1024)
-VECTOR_FETCH_CUTS = (0, 256, 448)
-SCALAR_FETCH_CUTS = (448, 768, 1024)
+VECTOR_FETCH_CUTS = (0, 256, 384)
+SCALAR_FETCH_CUTS = (384, 768, 1024)
 VECTOR_PUT = (256, 736)
+LOADED = 1280
 STORE_CUTS = (0, 368, 832, 1392, 2048)
 
 
@@ -70,10 +71,11 @@ def tile_picked_idxput_max_p_kernel(tc, x_words, x_scales, mem, w1, offs, slot, 
                 out=planes[j:P:ROWS, :].bitcast(I32),
                 in_=scales_picked[64 + PASSES * j : 64 + PASSES * j + QUAD, :].bitcast(I32),
             )
-        mem_scalar = windows.tile([P, U], F32, name="mem_scalar", offset=0, align_bytes=64)
-        nc.sync.dma_start(out=mem_scalar[:], in_=mem)
-        mem_vector = windows.tile([P, U], F32, name="mem_vector", offset=4 * U, align_bytes=64)
-        nc.sync.dma_start(out=mem_vector[:], in_=mem)
+        mem_first = windows.tile([P, U], F32, name="mem_first", offset=0, align_bytes=64)
+        nc.sync.dma_start(out=mem_first[:], in_=mem)
+        mem_second = windows.tile([P, U], F32, name="mem_second", offset=4 * U, align_bytes=64)
+        nc.sync.dma_start(out=mem_second[:, 0:LOADED], in_=mem[:, 0:LOADED])
+        nc.gpsimd.tensor_copy(mem_second[:, LOADED:U], mem_first[:, LOADED:U])
 
         first = keep.tile([P, S], U32, name="words_picked0", align_bytes=64)
         nc.vector.tensor_copy(first[:], words_all[0][:].indirect(offs_sb[:]))
@@ -82,10 +84,10 @@ def tile_picked_idxput_max_p_kernel(tc, x_words, x_scales, mem, w1, offs, slot, 
         w_scales = keep.tile([P, PASSES * N], U8, name="w_scales", align_bytes=64)
         second = []
         for z in range(PASSES):
-            half = keep.tile([P, HALF], U32, name="words_picked1_%d" % z, tag="staged%d" % z, align_bytes=64)
-            second.append(half)
-            a = z * HALF
-            nc.vector.tensor_copy(half[:], words_all[1][:].indirect(offs_sb[:, a // LANES : (a + HALF) // LANES]))
+            a, b = ((0, WORD_CUT), (WORD_CUT, S))[z]
+            part = keep.tile([P, b - a], U32, name="words_picked1_%d" % z, tag="staged%d" % z, align_bytes=64)
+            second.append(part)
+            nc.vector.tensor_copy(part[:], words_all[1][:].indirect(offs_sb[:, a // LANES : b // LANES]))
             w_grouped = keep.tile([P, N, PACK], BF16, name="w_grouped%d" % z, tag="staged%d" % (z + 1), align_bytes=64)
             nc.scalar.copy(
                 w_grouped[:].rearrange("p (c i) j -> p c j i", i=4),
@@ -99,9 +101,9 @@ def tile_picked_idxput_max_p_kernel(tc, x_words, x_scales, mem, w1, offs, slot, 
 
         old = keep.tile([P, S], F32, name="old")
         for a, b in zip(VECTOR_FETCH_CUTS, VECTOR_FETCH_CUTS[1:]):
-            nc.vector.tensor_copy(old[:, a:b], mem_scalar[:].indirect(slots(a, b)))
+            nc.vector.tensor_copy(old[:, a:b], mem_first[:].indirect(slots(a, b)))
         for a, b in zip(SCALAR_FETCH_CUTS, SCALAR_FETCH_CUTS[1:]):
-            nc.scalar.activation(old[:, a:b], mem_scalar[:].indirect(slots(a, b)), COPY)
+            nc.scalar.activation(old[:, a:b], mem_first[:].indirect(slots(a, b)), COPY)
 
         new = keep.tile([P, S], F32, name="new")
         banks = [(a, b, psum.tile([P, b - a], F32, name="bank%d" % a)) for a, b in zip(BANK_CUTS, BANK_CUTS[1:])]
@@ -120,17 +122,18 @@ def tile_picked_idxput_max_p_kernel(tc, x_words, x_scales, mem, w1, offs, slot, 
         for a, b, bank in banks:
             product(0, first[:, a:b], a, b, bank[:], False)
         for a, b, bank in banks:
-            for c in range(a, b, PIECE):
-                codes = second[c // HALF][:, c % HALF : c % HALF + PIECE]
-                product(1, codes, c, c + PIECE, bank[:, c - a : c - a + PIECE], c + PIECE == b)
+            for c, d in zip(PRODUCT_CUTS, PRODUCT_CUTS[1:]):
+                if a <= c < b:
+                    codes = second[c // WORD_CUT][:, c % WORD_CUT : c % WORD_CUT + d - c]
+                    product(1, codes, c, d, bank[:, c - a : d - a], d == b)
             nc.vector.tensor_tensor(new[:, a:b], bank[:], old[:, a:b], MAX)
 
         a, b = VECTOR_PUT
-        nc.scalar.activation(mem_scalar[:].indirect(slots(0, a)), new[:, 0:a], COPY)
-        nc.scalar.activation(mem_scalar[:].indirect(slots(b, S)), new[:, b:S], COPY)
-        nc.vector.tensor_copy(mem_vector[:].indirect(slots(a, b)), new[:, a:b])
+        nc.scalar.activation(mem_second[:].indirect(slots(0, a)), new[:, 0:a], COPY)
+        nc.scalar.activation(mem_second[:].indirect(slots(b, S)), new[:, b:S], COPY)
+        nc.vector.tensor_copy(mem_first[:].indirect(slots(a, b)), new[:, a:b])
 
         merged = keep.tile([P, U], F32, name="merged")
         for a, b in zip(STORE_CUTS, STORE_CUTS[1:]):
-            nc.vector.tensor_tensor(merged[:, a:b], mem_scalar[:, a:b], mem_vector[:, a:b], MAX)
+            nc.vector.tensor_tensor(merged[:, a:b], mem_first[:, a:b], mem_second[:, a:b], MAX)
             nc.sync.dma_start(out=out[:, a:b], in_=merged[:, a:b])

@@ -28,7 +28,7 @@ BANK_CUTS = (0, 256, 768, 1024)
 VECTOR_FETCH_CUTS = (0, 256, 384)
 SCALAR_FETCH_CUTS = (384, 768, 1024)
 VECTOR_PUT = (256, 736)
-LOADED = 1280
+LOADED = 1408
 STORE_CUTS = (0, 368, 832, 1392, 2048)
 
 

@@ -29,7 +29,7 @@ VECTOR_FETCH_CUTS = (0, 256, 384)
 SCALAR_FETCH_CUTS = (384, 768, 1024)
 VECTOR_PUT = (256, 736)
 LOADED = 1408
-STORE_CUTS = (0, 368, 832, 1392, 2048)
+STORE_CUTS = (0, 320, 848, 1472, 2048)
 
 
 def tile_picked_idxput_max_p_kernel(tc, x_words, x_scales, mem, w1, offs, slot, out):

from contextlib import ExitStack

import concourse.mybir as mybir

K, T, S, N, U = 1024, 2048, 1024, 128, 2048
FLOPS = 2 * K * N * S

F32 = mybir.dt.float32
BF16 = mybir.dt.bfloat16
I32 = mybir.dt.int32
U32 = mybir.dt.uint32
U16 = mybir.dt.uint16
U8 = mybir.dt.uint8
FP8X4 = mybir.dt.float8_e4m3fn_x4
COPY = mybir.ActivationFunctionType.Copy
MAX = mybir.AluOpType.max

P = 128
PACK = 4
PASSES = K // (P * PACK)
LANES = 16
QUAD = 32
ROWS = 4
PLANE_ROW = (0, 4)
WORD_CUT = 640
PRODUCT_CUTS = (0, 256, 512, 640, 768, 1024)
BANK_CUTS = (0, 256, 768, 1024)
VECTOR_FETCH_CUTS = (0, 256, 384)
SCALAR_FETCH_CUTS = (384, 768, 1024)
VECTOR_PUT = (256, 736)
LOADED = 1408
STORE_CUTS = (0, 320, 848, 1472, 2048)


def tile_picked_idxput_max_p_kernel(tc, x_words, x_scales, mem, w1, offs, slot, out):
    nc = tc.nc
    with ExitStack() as ctx:
        keep = ctx.enter_context(tc.tile_pool(name="keep", bufs=1))
        windows = ctx.enter_context(tc.tile_pool(name="windows", bufs=1))
        psum = ctx.enter_context(tc.psum_pool(name="psum", bufs=1))

        offs_sb = keep.tile([P, S // LANES], U16, name="offs_sb")
        slot_sb = keep.tile([P, S // LANES], U16, name="slot_sb")

        def slots(a, b):
            return slot_sb[:, a // LANES : b // LANES]

        scales_all = windows.tile([P, T], U8, name="scales_all", offset=4 * U - T // 2, align_bytes=64)
        words_all = [keep.tile([P, T], U32, name="words_all%d" % z, align_bytes=64) for z in range(PASSES)]
        w_raw = keep.tile([P, PASSES, PACK, N], F32, name="w_raw", align_bytes=64)

        nc.vector.memset(scales_all[0:64, :].bitcast(I32), 0)
        nc.vector.memset(scales_all[96:P, :].bitcast(I32), 0)
        x_rows = x_words.rearrange("z p n t -> z p (n t)").bitcast(I32)
        nc.sync.dma_start(
            out=scales_all[64:96, :].bitcast(I32),
            in_=x_scales.bitcast(I32).rearrange("z r n -> r z n"),
        )
        nc.sync.dma_start(offs_sb[:], offs)
        for z in range(PASSES):
            nc.sync.dma_start(out=words_all[z][:].bitcast(I32), in_=x_rows[z])
        nc.sync.dma_start(out=w_raw[:], in_=w1.rearrange("(z p j) m -> p z j m", z=PASSES, j=PACK))
        nc.sync.dma_start(slot_sb[:], slot)

        scales_picked = keep.tile([P, S], U8, name="scales_picked", align_bytes=64)
        nc.vector.tensor_copy(scales_picked[:], scales_all[:].indirect(offs_sb[:]))

        planes = keep.tile([P, S], U8, name="planes", align_bytes=64)
        for j in range(ROWS):
            nc.sync.dma_start(
                out=planes[j:P:ROWS, :].bitcast(I32),
                in_=scales_picked[64 + PASSES * j : 64 + PASSES * j + QUAD, :].bitcast(I32),
            )
        mem_first = windows.tile([P, U], F32, name="mem_first", offset=0, align_bytes=64)
        nc.sync.dma_start(out=mem_first[:], in_=mem)
        mem_second = windows.tile([P, U], F32, name="mem_second", offset=4 * U, align_bytes=64)
        nc.sync.dma_start(out=mem_second[:, 0:LOADED], in_=mem[:, 0:LOADED])
        nc.gpsimd.tensor_copy(mem_second[:, LOADED:U], mem_first[:, LOADED:U])

        first = keep.tile([P, S], U32, name="words_picked0", align_bytes=64)
        nc.vector.tensor_copy(first[:], words_all[0][:].indirect(offs_sb[:]))

        w_codes = keep.tile([P, PASSES * N], U32, name="w_codes", align_bytes=64)
        w_scales = keep.tile([P, PASSES * N], U8, name="w_scales", align_bytes=64)
        second = []
        for z in range(PASSES):
            a, b = ((0, WORD_CUT), (WORD_CUT, S))[z]
            part = keep.tile([P, b - a], U32, name="words_picked1_%d" % z, tag="staged%d" % z, align_bytes=64)
            second.append(part)
            nc.vector.tensor_copy(part[:], words_all[1][:].indirect(offs_sb[:, a // LANES : b // LANES]))
            w_grouped = keep.tile([P, N, PACK], BF16, name="w_grouped%d" % z, tag="staged%d" % (z + 1), align_bytes=64)
            nc.scalar.copy(
                w_grouped[:].rearrange("p (c i) j -> p c j i", i=4),
                w_raw[:, z].rearrange("p j (c i) -> p c j i", i=4),
            )
            nc.vector.quantize_mx(
                out=w_codes[:, z * N : (z + 1) * N].bitcast(FP8X4),
                scales=w_scales[:, z * N : (z + 1) * N],
                in_=w_grouped[:].rearrange("p m j -> p (m j)"),
            )

        old = keep.tile([P, S], F32, name="old")
        for a, b in zip(VECTOR_FETCH_CUTS, VECTOR_FETCH_CUTS[1:]):
            nc.vector.tensor_copy(old[:, a:b], mem_first[:].indirect(slots(a, b)))
        for a, b in zip(SCALAR_FETCH_CUTS, SCALAR_FETCH_CUTS[1:]):
            nc.scalar.activation(old[:, a:b], mem_first[:].indirect(slots(a, b)), COPY)

        new = keep.tile([P, S], F32, name="new")
        banks = [(a, b, psum.tile([P, b - a], F32, name="bank%d" % a)) for a, b in zip(BANK_CUTS, BANK_CUTS[1:])]

        def product(z, codes, a, b, into, last):
            nc.tensor.matmul_mx(
                out=into,
                lhsT=w_codes[:, z * N : (z + 1) * N].bitcast(FP8X4),
                lhsT_scale=w_scales[:, z * N : (z + 1) * N],
                rhs=codes.bitcast(FP8X4),
                rhs_scale=planes[PLANE_ROW[z] : P, a:b],
                start=(z == 0),
                stop=last,
            )

        for a, b, bank in banks:
            product(0, first[:, a:b], a, b, bank[:], False)
        for a, b, bank in banks:
            for c, d in zip(PRODUCT_CUTS, PRODUCT_CUTS[1:]):
                if a <= c < b:
                    codes = second[c // WORD_CUT][:, c % WORD_CUT : c % WORD_CUT + d - c]
                    product(1, codes, c, d, bank[:, c - a : d - a], d == b)
            nc.vector.tensor_tensor(new[:, a:b], bank[:], old[:, a:b], MAX)

        a, b = VECTOR_PUT
        nc.scalar.activation(mem_second[:].indirect(slots(0, a)), new[:, 0:a], COPY)
        nc.scalar.activation(mem_second[:].indirect(slots(b, S)), new[:, b:S], COPY)
        nc.vector.tensor_copy(mem_first[:].indirect(slots(a, b)), new[:, a:b])

        merged = keep.tile([P, U], F32, name="merged")
        for a, b in zip(STORE_CUTS, STORE_CUTS[1:]):
            nc.vector.tensor_tensor(merged[:, a:b], mem_first[:, a:b], mem_second[:, a:b], MAX)
            nc.sync.dma_start(out=out[:, a:b], in_=merged[:, a:b])
